import numpy as np
import ml_dtypes


def mxq(x, axis, fmt="e4m3"):
    dtype, down = {"e4m3": (ml_dtypes.float8_e4m3fn, 7), "e5m2": (ml_dtypes.float8_e5m2, 14)}[fmt]
    v = np.moveaxis(np.asarray(x, np.float32).astype(ml_dtypes.bfloat16).astype(np.float64), axis, -1)
    blocks = v.reshape(v.shape[:-1] + (-1, 32))
    amax = np.abs(blocks).max(-1, keepdims=True)
    byte = np.maximum(np.where(amax > 0, np.frexp(amax)[1] - 1 + 127, 0) - down, 1)
    scale = np.exp2(byte - 127.0)
    codes = (blocks / scale).astype(np.float32).astype(dtype).astype(np.float64)
    return np.moveaxis((codes * scale).reshape(v.shape), -1, axis)


WIDE = False


def mx_kscale(k):
    if not WIDE:
        return np.ones(k)
    levels = np.array([30, -30])
    if k % 512:
        return np.exp2(np.random.permutation(np.resize(levels, k // 32))).repeat(32)
    a = np.empty((k // 512, 16))
    for p in range(k // 512):
        a[p, :8] = np.random.permutation(np.resize(levels, 8))
        for g in range(8):
            far = levels[np.abs(levels - a[p, g]) >= 10]
            a[p, g + 8] = far[np.random.randint(len(far))]
    return np.exp2(a.ravel()).repeat(32)


def f64(x):
    return np.asarray(x).astype(np.float64)


def striped(idx):
    return np.tile(np.asarray(idx).reshape(-1, 16).T, (8, 1)).astype(np.uint16)


def unstriped(offs):
    return offs[:16].T.reshape(-1).astype(np.int64)


E2M1 = np.array([0.0, 0.5, 1.0, 1.5, 2.0, 3.0, 4.0, 6.0, -0.0, -0.5, -1.0, -1.5, -2.0, -3.0, -4.0, -6.0])


def pack_weight(w, fmt):
    k, n = w.shape
    w = f64(np.asarray(w, np.float32).astype(ml_dtypes.bfloat16)).reshape(k // 32, 32, n)
    amax = np.abs(w).max(1)
    if fmt in ("e4m3", "e5m2"):
        byte = np.frexp(amax)[1] - 1 + 127 - (7 if fmt == "e4m3" else 14)
    else:
        mant, ex = np.frexp(amax / 6.0)
        byte = np.where(mant > 0.5, ex, ex - 1) + 127
    byte = np.clip(np.where(amax > 0, byte, 1), 1, 254)
    scaled = (w * np.exp2(127.0 - byte)[:, None, :]).reshape(k, n).astype(np.float32)
    by_word = np.ascontiguousarray(scaled.reshape(k // 512, 128, 4, n).transpose(0, 1, 3, 2))
    if fmt in ("e4m3", "e5m2"):
        words = by_word.astype(ml_dtypes.float8_e4m3fn if fmt == "e4m3" else ml_dtypes.float8_e5m2).view(np.uint8)
    else:
        c = by_word.astype(ml_dtypes.float4_e2m1fn).view(np.uint8) & 0xF
        words = (c[..., 0::2] | (c[..., 1::2] << 4)).reshape(k // 512, 128, 2 * n)
    return np.ascontiguousarray(words), np.ascontiguousarray(byte.astype(np.uint8).reshape(k // 512, 16, n))


def unpack_weight(words, scales, fmt):
    g, _, n = scales.shape
    words = np.ascontiguousarray(words).reshape(g, 128, n, -1)
    if fmt in ("e4m3", "e5m2"):
        vals = words.view(ml_dtypes.float8_e4m3fn if fmt == "e4m3" else ml_dtypes.float8_e5m2).astype(np.float64)
    else:
        nib = np.empty((g, 128, n, 4), np.uint8)
        nib[..., 0::2] = words & 0xF
        nib[..., 1::2] = words >> 4
        vals = E2M1[nib]
    vals = vals * np.repeat(np.exp2(scales.astype(np.float64) - 127.0), 8, axis=1)[..., None]
    return vals.transpose(0, 1, 3, 2).reshape(g * 512, n)


K, T, J, I, C = 1024, 1024, 256, 256, 1024


def setup_inputs():
    n = np.random.standard_normal
    idx = np.random.permutation(T)[:J]
    idx2 = np.random.permutation(T)[:J]
    idx3 = np.random.permutation(C)[:I]
    fk = mx_kscale(K)
    kyp = pack_weight(n((K, I)) / fk[:, None], "e5m2")
    return {
        "xf": (n((K, T)) * 0.03).astype(np.float32),
        "fk": (np.random.uniform(0.5, 2.0, (K, 1)) * fk[:, None]).astype(np.float32),
        "ky_words": kyp[0],
        "ky_scales": kyp[1],
        "bi": (np.random.uniform(-0.7, 0.7, (1, I))).astype(np.float32),
        "old": (1.0 * n((J, C))).astype(np.float32),
        "offs": striped(idx),
        "offs2": striped(idx2),
        "offs3": striped(idx3),
    }


def reference(xf, fk, ky_words, ky_scales, bi, old, offs, offs2, offs3):
    idx = unstriped(offs)
    idx2 = unstriped(offs2)
    idx3 = unstriped(offs3)
    kyu = unpack_weight(ky_words, ky_scales, "e5m2")
    u = (f64(xf)[:, idx] - f64(xf)[:, idx2]) * f64(fk)
    uq = mxq(u, 0, "e5m2")
    a0 = uq.T @ kyu
    a = a0 + f64(bi)
    pp = np.zeros((J, C))
    pp[:, idx3] = a
    y = np.maximum(pp, f64(old))
    return y

@@ -1,0 +1,123 @@
+from contextlib import ExitStack
+
+import concourse.mybir as mybir
+from concourse.masks import make_identity
+
+K, T, J, I, C = 1024, 1024, 256, 256, 1024
+FLOPS = 2 * K * J * I
+
+F32 = mybir.dt.float32
+BF16 = mybir.dt.bfloat16
+I32 = mybir.dt.int32
+U32 = mybir.dt.uint32
+U16 = mybir.dt.uint16
+U8 = mybir.dt.uint8
+E5M2X4 = mybir.dt.float8_e5m2_x4
+COPY = mybir.ActivationFunctionType.Copy
+ALU = mybir.AluOpType
+
+P = 128
+PACK = 4
+PASSES = K // (P * PACK)
+HALVES = J // P
+LIST_COLS = P // 16
+STORE_COLS = 512
+
+
+def tile_list_scores_gaps_given_placed_kernel(tc, xf, fk, ky_words, ky_scales, bi, old, offs, offs2, offs3, out):
+    nc = tc.nc
+    with ExitStack() as ctx:
+        keep = ctx.enter_context(tc.tile_pool(name="keep", bufs=1))
+        psum = ctx.enter_context(tc.psum_pool(name="psum", bufs=1))
+
+        rows_a = keep.tile([P, J // 16], U16, name="rows_a")
+        rows_b = keep.tile([P, J // 16], U16, name="rows_b")
+        places = keep.tile([P, I // 16], U16, name="places")
+        planes = [keep.tile([P, T], F32, name=f"plane{q}") for q in range(PASSES * PACK)]
+        factors = keep.tile([P, PASSES, PACK], F32, name="factors")
+        bias_cols = keep.tile([P, 2], F32, name="bias_cols")
+        key_codes = keep.tile([P, PASSES, I], U32, name="key_codes", align_bytes=64)
+        key_scales = keep.tile([P, PASSES, I], U8, name="key_scales", align_bytes=64)
+        olds = [keep.tile([P, C], F32, name=f"old{h}") for h in range(HALVES)]
+        pages = [keep.tile([P, C], F32, name=f"page{h}") for h in range(HALVES)]
+
+        nc.vector.memset(key_scales[:].rearrange("p z n -> p (z n)").bitcast(I32), 0)
+        for h in range(HALVES):
+            nc.vector.memset(pages[h][:], 0.0)
+
+        xf_planes = xf.rearrange("(a p t) n -> a t p n", a=PASSES, t=PACK)
+        nc.sync.dma_start(planes[0][:], xf_planes[0, 0])
+        nc.sync.dma_start(rows_b[:], offs2)
+        nc.sync.dma_start(rows_a[:], offs)
+        nc.scalar.dma_start(factors[:], fk.rearrange("(a p t) o -> p a (t o)", a=PASSES, t=PACK))
+        nc.scalar.dma_start(bias_cols[:], bi.rearrange("o (p m) -> p (o m)", m=2))
+        for q in range(1, PASSES * PACK):
+            nc.sync.dma_start(planes[q][:], xf_planes[q // PACK, q % PACK])
+        nc.sync.dma_start(key_codes[:].bitcast(I32), ky_words.rearrange("z p n t -> p z (n t)").bitcast(I32))
+        for quad in range(4):
+            nc.sync.dma_start(
+                key_scales[32 * quad : 32 * quad + 4].bitcast(I32),
+                ky_scales[:, 4 * quad : 4 * quad + 4, :].rearrange("z r n -> r z n").bitcast(I32),
+            )
+        nc.sync.dma_start(places[:], offs3)
+        for h in range(HALVES):
+            nc.sync.dma_start(olds[h][:], old[h * P : (h + 1) * P, :])
+
+        identity = keep.tile([P, P], F32, name="identity")
+        make_identity(nc, identity[:])
+        bias_bank = psum.tile([P, 2, P], F32, name="bias_bank")
+        for m in range(2):
+            nc.tensor.transpose(bias_bank[:, m, :], bias_cols[:, m : m + 1].to_broadcast([P, P]), identity[:])
+        bias = keep.tile([P, I], F32, name="bias")
+        nc.scalar.copy(bias[:].rearrange("p (n m) -> p n m", m=2), bias_bank[:].rearrange("p m n -> p n m"))
+
+        banks = [psum.tile([P, I], F32, name=f"bank{h}") for h in range(HALVES)]
+        first, second = slice(0, P), slice(P, 2 * P)
+        first_offs, second_offs = slice(0, LIST_COLS), slice(LIST_COLS, 2 * LIST_COLS)
+        for a in range(PASSES):
+            woven = [keep.tile([P, P * PACK], BF16, name=f"woven{a}_{h}", align_bytes=64) for h in range(HALVES)]
+            for t in range(PACK):
+                plane = planes[a * PACK + t]
+                tag = f"{a}_{t}"
+                sub0 = keep.tile([P, P], F32, name="sub0_" + tag)
+                sub1 = keep.tile([P, P], F32, name="sub1_" + tag)
+                min1 = keep.tile([P, P], F32, name="min1_" + tag)
+                gap0 = keep.tile([P, P], F32, name="gap0_" + tag)
+                gap1 = keep.tile([P, P], F32, name="gap1_" + tag)
+                nc.scalar.activation(sub0[:], plane[:].indirect(rows_b[:, first_offs]), COPY)
+                nc.scalar.activation(sub1[:], plane[:].indirect(rows_b[:, second_offs]), COPY)
+                nc.scalar.activation(min1[:], plane[:].indirect(rows_a[:, second_offs]), COPY)
+                nc.vector.tensor_tensor(gap0[:], plane[:].indirect(rows_a[:, first_offs]), sub0[:], ALU.subtract)
+                nc.vector.tensor_scalar(
+                    woven[0][:].rearrange("p (j t) -> p j t", t=PACK)[:, :, t], gap0[:], factors[:, a, t : t + 1], None, ALU.mult
+                )
+                nc.vector.tensor_tensor(gap1[:], min1[:], sub1[:], ALU.subtract)
+                nc.vector.tensor_scalar(
+                    woven[1][:].rearrange("p (j t) -> p j t", t=PACK)[:, :, t], gap1[:], factors[:, a, t : t + 1], None, ALU.mult
+                )
+            for h in range(HALVES):
+                codes = keep.tile([P, P], U32, name=f"codes{a}_{h}", align_bytes=64)
+                scales = keep.tile([P, P], U8, name=f"scales{a}_{h}", align_bytes=64)
+                nc.vector.quantize_mx(out=codes[:].bitcast(E5M2X4), scales=scales[:], in_=woven[h][:])
+                nc.tensor.matmul_mx(
+                    out=banks[h][:],
+                    lhsT=codes[:].bitcast(E5M2X4),
+                    lhsT_scale=scales[:],
+                    rhs=key_codes[:, a, :].bitcast(E5M2X4),
+                    rhs_scale=key_scales[:, a, :],
+                    start=(a == 0),
+                    stop=(a == PASSES - 1),
+                )
+
+        scores = [keep.tile([P, I], F32, name=f"scores{h}") for h in range(HALVES)]
+        for h in range(HALVES):
+            nc.vector.tensor_tensor(scores[h][:], banks[h][:], bias[:], ALU.add)
+        nc.scalar.activation(pages[0][:].indirect(places[:]), scores[0][:], COPY)
+        nc.vector.tensor_copy(pages[1][:].indirect(places[:, first_offs]), scores[1][:, first])
+        nc.scalar.activation(pages[1][:].indirect(places[:, second_offs]), scores[1][:, second], COPY)
+        for h in range(HALVES):
+            result = keep.tile([P, C], F32, name=f"result{h}")
+            for c0 in range(0, C, STORE_COLS):
+                cols = slice(c0, c0 + STORE_COLS)
+                nc.vector.tensor_tensor(result[:, cols], pages[h][:, cols], olds[h][:, cols], ALU.max)
+                nc.sync.dma_start(out[h * P : (h + 1) * P, cols], result[:, cols])

@@ -34,7 +34,7 @@ def tile_list_scores_gaps_given_placed_kernel(tc, xf, fk, ky_words, ky_scales, b
         rows_b = keep.tile([P, J // 16], U16, name="rows_b")
         places = keep.tile([P, I // 16], U16, name="places")
         planes = [keep.tile([P, T], F32, name=f"plane{q}") for q in range(PASSES * PACK)]
-        factors = keep.tile([P, PASSES, PACK], F32, name="factors")
+        factors = [keep.tile([P, PACK], F32, name=f"factors{a}") for a in range(PASSES)]
         bias_cols = keep.tile([P, 2], F32, name="bias_cols")
         key_codes = keep.tile([P, PASSES, I], U32, name="key_codes", align_bytes=64)
         key_scales = keep.tile([P, PASSES, I], U8, name="key_scales", align_bytes=64)
@@ -49,10 +49,12 @@ def tile_list_scores_gaps_given_placed_kernel(tc, xf, fk, ky_words, ky_scales, b
         nc.sync.dma_start(planes[0][:], xf_planes[0, 0])
         nc.sync.dma_start(rows_b[:], offs2)
         nc.sync.dma_start(rows_a[:], offs)
-        nc.scalar.dma_start(factors[:], fk.rearrange("(a p t) o -> p a (t o)", a=PASSES, t=PACK))
-        nc.scalar.dma_start(bias_cols[:], bi.rearrange("o (p m) -> p (o m)", m=2))
+        fk_passes = fk.rearrange("(a p t) o -> a p (t o)", a=PASSES, t=PACK)
+        nc.scalar.dma_start(factors[0][:], fk_passes[0])
         for q in range(1, PASSES * PACK):
             nc.sync.dma_start(planes[q][:], xf_planes[q // PACK, q % PACK])
+        nc.sync.dma_start(factors[1][:], fk_passes[1])
+        nc.sync.dma_start(bias_cols[:], bi.rearrange("o (p m) -> p (o m)", m=2))
         nc.sync.dma_start(key_codes[:].bitcast(I32), ky_words.rearrange("z p n t -> p z (n t)").bitcast(I32))
         for quad in range(4):
             nc.sync.dma_start(
@@ -72,49 +74,79 @@ def tile_list_scores_gaps_given_placed_kernel(tc, xf, fk, ky_words, ky_scales, b
         nc.scalar.copy(bias[:].rearrange("p (n m) -> p n m", m=2), bias_bank[:].rearrange("p m n -> p n m"))
 
         banks = [psum.tile([P, I], F32, name=f"bank{h}") for h in range(HALVES)]
-        first, second = slice(0, P), slice(P, 2 * P)
-        first_offs, second_offs = slice(0, LIST_COLS), slice(LIST_COLS, 2 * LIST_COLS)
-        for a in range(PASSES):
-            woven = [keep.tile([P, P * PACK], BF16, name=f"woven{a}_{h}", align_bytes=64) for h in range(HALVES)]
-            for t in range(PACK):
-                plane = planes[a * PACK + t]
-                tag = f"{a}_{t}"
-                sub0 = keep.tile([P, P], F32, name="sub0_" + tag)
-                sub1 = keep.tile([P, P], F32, name="sub1_" + tag)
-                min1 = keep.tile([P, P], F32, name="min1_" + tag)
-                gap0 = keep.tile([P, P], F32, name="gap0_" + tag)
-                gap1 = keep.tile([P, P], F32, name="gap1_" + tag)
-                nc.scalar.activation(sub0[:], plane[:].indirect(rows_b[:, first_offs]), COPY)
-                nc.scalar.activation(sub1[:], plane[:].indirect(rows_b[:, second_offs]), COPY)
-                nc.scalar.activation(min1[:], plane[:].indirect(rows_a[:, second_offs]), COPY)
-                nc.vector.tensor_tensor(gap0[:], plane[:].indirect(rows_a[:, first_offs]), sub0[:], ALU.subtract)
-                nc.vector.tensor_scalar(
-                    woven[0][:].rearrange("p (j t) -> p j t", t=PACK)[:, :, t], gap0[:], factors[:, a, t : t + 1], None, ALU.mult
-                )
-                nc.vector.tensor_tensor(gap1[:], min1[:], sub1[:], ALU.subtract)
-                nc.vector.tensor_scalar(
-                    woven[1][:].rearrange("p (j t) -> p j t", t=PACK)[:, :, t], gap1[:], factors[:, a, t : t + 1], None, ALU.mult
-                )
-            for h in range(HALVES):
-                codes = keep.tile([P, P], U32, name=f"codes{a}_{h}", align_bytes=64)
-                scales = keep.tile([P, P], U8, name=f"scales{a}_{h}", align_bytes=64)
-                nc.vector.quantize_mx(out=codes[:].bitcast(E5M2X4), scales=scales[:], in_=woven[h][:])
-                nc.tensor.matmul_mx(
-                    out=banks[h][:],
-                    lhsT=codes[:].bitcast(E5M2X4),
-                    lhsT_scale=scales[:],
-                    rhs=key_codes[:, a, :].bitcast(E5M2X4),
-                    rhs_scale=key_scales[:, a, :],
-                    start=(a == 0),
-                    stop=(a == PASSES - 1),
-                )
+        halves = [slice(h * P, (h + 1) * P) for h in range(HALVES)]
+        half_offs = [slice(h * LIST_COLS, (h + 1) * LIST_COLS) for h in range(HALVES)]
 
+        def walk(woven):
+            return woven[:].rearrange("p (c i t) -> p c t i", i=4, t=PACK)
+
+        def scale_and_weave(a, woven, gaps, slots):
+            width = gaps.shape[2]
+            count = slots.stop - slots.start
+            nc.vector.tensor_tensor(
+                walk(woven)[:, :, slots, :],
+                gaps[:, slots, :].rearrange("p t (c i) -> p c t i", i=4),
+                factors[a][:, slots].unsqueeze(1).unsqueeze(3).to_broadcast([P, width // 4, count, 4]),
+                ALU.mult,
+            )
+
+        def quantise(woven, name):
+            width = woven.shape[1] // PACK
+            codes = keep.tile([P, width], U32, name="codes" + name, align_bytes=64)
+            scales = keep.tile([P, width], U8, name="scales" + name, align_bytes=64)
+            nc.vector.quantize_mx(out=codes[:].bitcast(E5M2X4), scales=scales[:], in_=woven[:])
+            return codes, scales
+
+        def multiply(a, h, codes, scales):
+            nc.tensor.matmul_mx(
+                out=banks[h][:],
+                lhsT=codes.bitcast(E5M2X4),
+                lhsT_scale=scales,
+                rhs=key_codes[:, a, :].bitcast(E5M2X4),
+                rhs_scale=key_scales[:, a, :],
+                start=(a == 0),
+                stop=(a == PASSES - 1),
+            )
+
+        gaps = [keep.tile([P, PACK, J], F32, name=f"gaps{a}") for a in range(PASSES)]
+        woven = [[keep.tile([P, P * PACK], BF16, name=f"woven{a}_{h}", align_bytes=64) for h in range(HALVES)] for a in range(PASSES)]
+        every_slot = slice(0, PACK)
+
+        def finish(a, h):
+            codes, scales = quantise(woven[a][h], f"{a}_{h}")
+            multiply(a, h, codes[:], scales[:])
+
+        for q in range(PASSES * PACK - 1):
+            a, t = divmod(q, PACK)
+            sub = keep.tile([P, J], F32, name=f"sub{q}")
+            nc.scalar.activation(sub[:], planes[q][:].indirect(rows_b[:]), COPY)
+            nc.vector.tensor_tensor(gaps[a][:, t, :], planes[q][:].indirect(rows_a[:]), sub[:], ALU.subtract)
+            if q == PACK - 1:
+                scale_and_weave(0, woven[0][0], gaps[0][:, :, halves[0]], every_slot)
+                finish(0, 0)
+
+        last = planes[-1]
         scores = [keep.tile([P, I], F32, name=f"scores{h}") for h in range(HALVES)]
         for h in range(HALVES):
-            nc.vector.tensor_tensor(scores[h][:], banks[h][:], bias[:], ALU.add)
+            sub = keep.tile([P, P], F32, name=f"last_sub{h}", tag=f"staging{h}")
+            nc.scalar.activation(sub[:], last[:].indirect(rows_b[:, half_offs[h]]), COPY)
+            nc.vector.tensor_tensor(gaps[1][:, PACK - 1, halves[h]], last[:].indirect(rows_a[:, half_offs[h]]), sub[:], ALU.subtract)
+
+        scale_and_weave(1, woven[1][0], gaps[1][:, :, halves[0]], every_slot)
+        finish(1, 0)
+        nc.vector.tensor_tensor(scores[0][:], banks[0][:], bias[:], ALU.add)
+
+        scaled = keep.tile([P, PACK, P], BF16, name="scaled", tag="staging0")
+        for t in range(PACK):
+            nc.scalar.activation(scaled[:, t, :], gaps[0][:, t, halves[1]], COPY, scale=factors[0][:, t : t + 1])
+        nc.scalar.copy(walk(woven[0][1]), scaled[:].rearrange("p t (c i) -> p c t i", i=4))
+        finish(0, 1)
+        scale_and_weave(1, woven[1][1], gaps[1][:, :, halves[1]], every_slot)
+        finish(1, 1)
+        nc.vector.tensor_tensor(scores[1][:], banks[1][:], bias[:], ALU.add)
         nc.scalar.activation(pages[0][:].indirect(places[:]), scores[0][:], COPY)
-        nc.vector.tensor_copy(pages[1][:].indirect(places[:, first_offs]), scores[1][:, first])
-        nc.scalar.activation(pages[1][:].indirect(places[:, second_offs]), scores[1][:, second], COPY)
+        nc.vector.tensor_copy(pages[1][:].indirect(places[:, half_offs[0]]), scores[1][:, halves[0]])
+        nc.scalar.activation(pages[1][:].indirect(places[:, half_offs[1]]), scores[1][:, halves[1]], COPY)
         for h in range(HALVES):
             result = keep.tile([P, C], F32, name=f"result{h}")
             for c0 in range(0, C, STORE_COLS):

from contextlib import ExitStack

import concourse.mybir as mybir
from concourse.masks import make_identity

K, T, J, I, C = 1024, 1024, 256, 256, 1024
FLOPS = 2 * K * J * I

F32 = mybir.dt.float32
BF16 = mybir.dt.bfloat16
I32 = mybir.dt.int32
U32 = mybir.dt.uint32
U16 = mybir.dt.uint16
U8 = mybir.dt.uint8
E5M2X4 = mybir.dt.float8_e5m2_x4
COPY = mybir.ActivationFunctionType.Copy
ALU = mybir.AluOpType

P = 128
PACK = 4
PASSES = K // (P * PACK)
HALVES = J // P
LIST_COLS = P // 16
STORE_COLS = 512


def tile_list_scores_gaps_given_placed_kernel(tc, xf, fk, ky_words, ky_scales, bi, old, offs, offs2, offs3, out):
    nc = tc.nc
    with ExitStack() as ctx:
        keep = ctx.enter_context(tc.tile_pool(name="keep", bufs=1))
        psum = ctx.enter_context(tc.psum_pool(name="psum", bufs=1))

        rows_a = keep.tile([P, J // 16], U16, name="rows_a")
        rows_b = keep.tile([P, J // 16], U16, name="rows_b")
        places = keep.tile([P, I // 16], U16, name="places")
        planes = [keep.tile([P, T], F32, name=f"plane{q}") for q in range(PASSES * PACK)]
        factors = [keep.tile([P, PACK], F32, name=f"factors{a}") for a in range(PASSES)]
        bias_cols = keep.tile([P, 2], F32, name="bias_cols")
        key_codes = keep.tile([P, PASSES, I], U32, name="key_codes", align_bytes=64)
        key_scales = keep.tile([P, PASSES, I], U8, name="key_scales", align_bytes=64)
        olds = [keep.tile([P, C], F32, name=f"old{h}") for h in range(HALVES)]
        pages = [keep.tile([P, C], F32, name=f"page{h}") for h in range(HALVES)]

        nc.vector.memset(key_scales[:].rearrange("p z n -> p (z n)").bitcast(I32), 0)
        for h in range(HALVES):
            nc.vector.memset(pages[h][:], 0.0)

        xf_planes = xf.rearrange("(a p t) n -> a t p n", a=PASSES, t=PACK)
        nc.sync.dma_start(planes[0][:], xf_planes[0, 0])
        nc.sync.dma_start(rows_b[:], offs2)
        nc.sync.dma_start(rows_a[:], offs)
        fk_passes = fk.rearrange("(a p t) o -> a p (t o)", a=PASSES, t=PACK)
        nc.scalar.dma_start(factors[0][:], fk_passes[0])
        for q in range(1, PASSES * PACK):
            nc.sync.dma_start(planes[q][:], xf_planes[q // PACK, q % PACK])
        nc.sync.dma_start(factors[1][:], fk_passes[1])
        nc.sync.dma_start(bias_cols[:], bi.rearrange("o (p m) -> p (o m)", m=2))
        nc.sync.dma_start(key_codes[:].bitcast(I32), ky_words.rearrange("z p n t -> p z (n t)").bitcast(I32))
        for quad in range(4):
            nc.sync.dma_start(
                key_scales[32 * quad : 32 * quad + 4].bitcast(I32),
                ky_scales[:, 4 * quad : 4 * quad + 4, :].rearrange("z r n -> r z n").bitcast(I32),
            )
        nc.sync.dma_start(places[:], offs3)
        for h in range(HALVES):
            nc.sync.dma_start(olds[h][:], old[h * P : (h + 1) * P, :])

        identity = keep.tile([P, P], F32, name="identity")
        make_identity(nc, identity[:])
        bias_bank = psum.tile([P, 2, P], F32, name="bias_bank")
        for m in range(2):
            nc.tensor.transpose(bias_bank[:, m, :], bias_cols[:, m : m + 1].to_broadcast([P, P]), identity[:])
        bias = keep.tile([P, I], F32, name="bias")
        nc.scalar.copy(bias[:].rearrange("p (n m) -> p n m", m=2), bias_bank[:].rearrange("p m n -> p n m"))

        banks = [psum.tile([P, I], F32, name=f"bank{h}") for h in range(HALVES)]
        halves = [slice(h * P, (h + 1) * P) for h in range(HALVES)]
        half_offs = [slice(h * LIST_COLS, (h + 1) * LIST_COLS) for h in range(HALVES)]

        def walk(woven):
            return woven[:].rearrange("p (c i t) -> p c t i", i=4, t=PACK)

        def scale_and_weave(a, woven, gaps, slots):
            width = gaps.shape[2]
            count = slots.stop - slots.start
            nc.vector.tensor_tensor(
                walk(woven)[:, :, slots, :],
                gaps[:, slots, :].rearrange("p t (c i) -> p c t i", i=4),
                factors[a][:, slots].unsqueeze(1).unsqueeze(3).to_broadcast([P, width // 4, count, 4]),
                ALU.mult,
            )

        def quantise(woven, name):
            width = woven.shape[1] // PACK
            codes = keep.tile([P, width], U32, name="codes" + name, align_bytes=64)
            scales = keep.tile([P, width], U8, name="scales" + name, align_bytes=64)
            nc.vector.quantize_mx(out=codes[:].bitcast(E5M2X4), scales=scales[:], in_=woven[:])
            return codes, scales

        def multiply(a, h, codes, scales):
            nc.tensor.matmul_mx(
                out=banks[h][:],
                lhsT=codes.bitcast(E5M2X4),
                lhsT_scale=scales,
                rhs=key_codes[:, a, :].bitcast(E5M2X4),
                rhs_scale=key_scales[:, a, :],
                start=(a == 0),
                stop=(a == PASSES - 1),
            )

        gaps = [keep.tile([P, PACK, J], F32, name=f"gaps{a}") for a in range(PASSES)]
        woven = [[keep.tile([P, P * PACK], BF16, name=f"woven{a}_{h}", align_bytes=64) for h in range(HALVES)] for a in range(PASSES)]
        every_slot = slice(0, PACK)

        def finish(a, h):
            codes, scales = quantise(woven[a][h], f"{a}_{h}")
            multiply(a, h, codes[:], scales[:])

        for q in range(PASSES * PACK - 1):
            a, t = divmod(q, PACK)
            sub = keep.tile([P, J], F32, name=f"sub{q}")
            nc.scalar.activation(sub[:], planes[q][:].indirect(rows_b[:]), COPY)
            nc.vector.tensor_tensor(gaps[a][:, t, :], planes[q][:].indirect(rows_a[:]), sub[:], ALU.subtract)
            if q == PACK - 1:
                scale_and_weave(0, woven[0][0], gaps[0][:, :, halves[0]], every_slot)
                finish(0, 0)

        last = planes[-1]
        scores = [keep.tile([P, I], F32, name=f"scores{h}") for h in range(HALVES)]
        for h in range(HALVES):
            sub = keep.tile([P, P], F32, name=f"last_sub{h}", tag=f"staging{h}")
            nc.scalar.activation(sub[:], last[:].indirect(rows_b[:, half_offs[h]]), COPY)
            nc.vector.tensor_tensor(gaps[1][:, PACK - 1, halves[h]], last[:].indirect(rows_a[:, half_offs[h]]), sub[:], ALU.subtract)

        scale_and_weave(1, woven[1][0], gaps[1][:, :, halves[0]], every_slot)
        finish(1, 0)
        nc.vector.tensor_tensor(scores[0][:], banks[0][:], bias[:], ALU.add)

        scaled = keep.tile([P, PACK, P], BF16, name="scaled", tag="staging0")
        for t in range(PACK):
            nc.scalar.activation(scaled[:, t, :], gaps[0][:, t, halves[1]], COPY, scale=factors[0][:, t : t + 1])
        nc.scalar.copy(walk(woven[0][1]), scaled[:].rearrange("p t (c i) -> p c t i", i=4))
        finish(0, 1)
        scale_and_weave(1, woven[1][1], gaps[1][:, :, halves[1]], every_slot)
        finish(1, 1)
        nc.vector.tensor_tensor(scores[1][:], banks[1][:], bias[:], ALU.add)
        nc.scalar.activation(pages[0][:].indirect(places[:]), scores[0][:], COPY)
        nc.vector.tensor_copy(pages[1][:].indirect(places[:, half_offs[0]]), scores[1][:, halves[0]])
        nc.scalar.activation(pages[1][:].indirect(places[:, half_offs[1]]), scores[1][:, halves[1]], COPY)
        for h in range(HALVES):
            result = keep.tile([P, C], F32, name=f"result{h}")
            for c0 in range(0, C, STORE_COLS):
                cols = slice(c0, c0 + STORE_COLS)
                nc.vector.tensor_tensor(result[:, cols], pages[h][:, cols], olds[h][:, cols], ALU.max)
                nc.sync.dma_start(out[h * P : (h + 1) * P, cols], result[:, cols])
